import numpy as np
import ml_dtypes


def mxq(x, axis, fmt="e4m3"):
    dtype, down = {"e4m3": (ml_dtypes.float8_e4m3fn, 7), "e5m2": (ml_dtypes.float8_e5m2, 14)}[fmt]
    v = np.moveaxis(np.asarray(x, np.float32).astype(ml_dtypes.bfloat16).astype(np.float64), axis, -1)
    blocks = v.reshape(v.shape[:-1] + (-1, 32))
    amax = np.abs(blocks).max(-1, keepdims=True)
    byte = np.maximum(np.where(amax > 0, np.frexp(amax)[1] - 1 + 127, 0) - down, 1)
    scale = np.exp2(byte - 127.0)
    codes = (blocks / scale).astype(np.float32).astype(dtype).astype(np.float64)
    return np.moveaxis((codes * scale).reshape(v.shape), -1, axis)


WIDE = False


def mx_kscale(k):
    if not WIDE:
        return np.ones(k)
    levels = np.array([10, -10, 5, -5, 0])
    if k % 512:
        return np.exp2(np.random.permutation(np.resize(levels, k // 32))).repeat(32)
    a = np.empty((k // 512, 16))
    for p in range(k // 512):
        a[p, :8] = np.random.permutation(np.resize(levels, 8))
        for g in range(8):
            far = levels[np.abs(levels - a[p, g]) >= 10]
            a[p, g + 8] = far[np.random.randint(len(far))]
    return np.exp2(a.ravel()).repeat(32)


def f64(x):
    return np.asarray(x).astype(np.float64)


def striped(idx):
    return np.tile(idx.reshape(-1, 16).T, (8, 1)).astype(np.uint16)


def unstriped(offs):
    return offs[:16].T.reshape(-1).astype(np.int64)


def striped8(idx):
    return np.concatenate([x.reshape(-1, 16).T for x in idx]).astype(np.uint16)


def runs(offs, k):
    lists = np.stack([offs[16 * r : 16 * r + 16].T.reshape(-1) for r in range(8)]).astype(np.int64)
    return lists[np.arange(k) % 512 // 64]


def pack_weight(w):
    k, n = w.shape
    w = f64(np.asarray(w, np.float32).astype(ml_dtypes.bfloat16)).reshape(k // 32, 32, n)
    amax = np.abs(w).max(1)
    byte = np.clip(np.where(amax > 0, np.frexp(amax)[1] - 1 + 127 - 7, 1), 1, 254)
    scaled = (w * np.exp2(127.0 - byte)[:, None, :]).reshape(k, n).astype(np.float32)
    words = np.ascontiguousarray(scaled.reshape(k // 512, 128, 4, n).transpose(0, 1, 3, 2)).astype(ml_dtypes.float8_e4m3fn).view(np.uint8)
    return words, np.ascontiguousarray(byte.astype(np.uint8).reshape(k // 512, 16, n))


def unpack_weight(words, scales):
    g, p, n, _ = words.shape
    vals = np.ascontiguousarray(words).view(ml_dtypes.float8_e4m3fn).astype(np.float64) * np.repeat(np.exp2(scales.astype(np.float64) - 127.0), 8, axis=1)[..., None]
    return vals.transpose(0, 1, 3, 2).reshape(g * 512, n)


def sigmoid(v):
    return 1.0 / (1.0 + np.exp(-np.maximum(v, -700.0)))


K, T, S, N, G, H, U = 512, 2048, 512, 512, 2048, 512, 1024


def setup_inputs():
    n = np.random.standard_normal
    s = mx_kscale(K)[:, None]
    u = mx_kscale(S)
    packed_xT = pack_weight(n((K, T)) * s)
    packed_dT = pack_weight(n((K, G)) / s)
    return {
        "x_words": packed_xT[0],
        "x_scales": packed_xT[1],
        "d_words": packed_dT[0],
        "d_scales": packed_dT[1],
        "gn": (np.random.uniform(0.5, 1.5, (H, 1)) * u[:, None]).astype(np.float32),
        "w1": (n((H, N)) / np.sqrt(H) / u[:, None]).astype(np.float32),
        "mem": n((N, U)).astype(np.float32),
        "offs": striped8(np.random.randint(0, T, (8, S))),
        "k1": striped8(np.random.randint(0, G, (8, H))),
        "n1": striped(np.random.permutation(S)),
        "n2": striped(np.random.permutation(U)[:S]),
    }


def reference(x_words, x_scales, d_words, d_scales, gn, w1, mem, offs, k1, n1, n2):
    old = f64(mem)[:, unstriped(n2)]
    d_k1 = unpack_weight(d_words, d_scales)[np.arange(K)[:, None], runs(k1, K)]
    xq = unpack_weight(x_words, x_scales)[np.arange(K)[:, None], runs(offs, K)]
    h = 0.0625 * (d_k1.T @ xq)
    st = h * (sigmoid(h[:, unstriped(n1)]))
    z = f64(gn) * (np.maximum(st, st[:, unstriped(n1)]))
    h2 = mxq(f64(w1), 0, "e4m3").T @ mxq(z, 0, "e4m3")
    nw = old + sigmoid(h2) * (h2 - old)
    out = f64(mem).copy()
    out[:, unstriped(n2)] = nw
    return out

@@ -1,0 +1,192 @@
+from contextlib import ExitStack
+
+import concourse.mybir as mybir
+
+F32 = mybir.dt.float32
+BF16 = mybir.dt.bfloat16
+I32 = mybir.dt.int32
+U32 = mybir.dt.uint32
+U16 = mybir.dt.uint16
+U8 = mybir.dt.uint8
+FP8X4 = mybir.dt.float8_e4m3fn_x4
+ALU = mybir.AluOpType
+ACT = mybir.ActivationFunctionType
+
+P = 128
+PACK = 4
+K, T, S, N, G, H, U = 512, 2048, 512, 512, 2048, 512, 1024
+HALF = S // 2
+LIST_COLS = S // 16
+FLOPS = 2 * K * H * S + 2 * H * N * S
+
+
+def half_cols(a):
+    return slice(a * HALF, (a + 1) * HALF)
+
+
+def half_list(lst, a):
+    return lst[:, a * LIST_COLS // 2 : (a + 1) * LIST_COLS // 2]
+
+
+def fetch(nc, on_scalar, out, window):
+    if on_scalar:
+        nc.scalar.activation(out=out, in_=window, func=ACT.Copy)
+    else:
+        nc.vector.tensor_copy(out=out, in_=window)
+
+
+def tile_picked_hpqtwicppaget_none_p_kernel(tc, x_words, x_scales, d_words, d_scales, gn, w1, mem, offs, k1, n1, n2, out):
+    nc = tc.nc
+    with ExitStack() as ctx:
+        keep = ctx.enter_context(tc.tile_pool(name="keep", bufs=1))
+        turns = ctx.enter_context(tc.tile_pool(name="turns", bufs=1))
+        psum = ctx.enter_context(tc.psum_pool(name="psum", bufs=1))
+
+        offs_sb = keep.tile([P, LIST_COLS], U16, name="offs_sb")
+        k1_sb = keep.tile([P, LIST_COLS], U16, name="k1_sb")
+        n1_sb = keep.tile([P, LIST_COLS], U16, name="n1_sb")
+        n2_sb = keep.tile([P, LIST_COLS], U16, name="n2_sb")
+
+        x_scale_tab = keep.tile([P, T], U8, name="x_scale_tab", align_bytes=64)
+        d_scale_tab = keep.tile([P, G], U8, name="d_scale_tab", align_bytes=64)
+        planes = keep.tile([P, S + H], U8, name="planes", align_bytes=64)
+        nc.vector.memset(x_scale_tab[:].bitcast(I32), 0)
+        nc.vector.memset(d_scale_tab[:].bitcast(I32), 0)
+        nc.vector.memset(planes[:].bitcast(I32), 0)
+
+        nc.sync.dma_start(offs_sb[:], offs)
+        nc.sync.dma_start(k1_sb[:], k1)
+        nc.sync.dma_start(n1_sb[:], n1)
+        nc.sync.dma_start(n2_sb[:], n2)
+        gain = keep.tile([P, PACK], F32, name="gain")
+        nc.sync.dma_start(gain[:], gn.rearrange("(p t) o -> p (t o)", t=PACK))
+        nc.sync.dma_start(x_scale_tab[0:P:8, :].bitcast(I32), x_scales[0].bitcast(I32))
+        nc.sync.dma_start(d_scale_tab[0:P:8, :].bitcast(I32), d_scales[0].bitcast(I32))
+        d_word_tab = turns.tile([P, G], U32, name="d_word_tab", offset=0)
+        x_word_tab = turns.tile([P, T], U32, name="x_word_tab", offset=8192)
+        nc.sync.dma_start(d_word_tab[:].bitcast(I32), d_words[0].rearrange("p n t -> p (n t)").bitcast(I32))
+        nc.sync.dma_start(x_word_tab[:].bitcast(I32), x_words[0].rearrange("p n t -> p (n t)").bitcast(I32))
+
+        picked_bytes = keep.tile([P, S + H], U8, name="picked_bytes", align_bytes=64)
+        nc.vector.tensor_copy(out=picked_bytes[:, :S], in_=x_scale_tab[:].indirect(offs_sb[:]))
+        nc.vector.tensor_copy(out=picked_bytes[:, S:], in_=d_scale_tab[:].indirect(k1_sb[:]))
+        for r in range(4):
+            nc.scalar.dma_start(planes[r:P:32, :].bitcast(I32), picked_bytes[8 * r : P : 32, :].bitcast(I32))
+
+        d_picked = turns.tile([P, H], U32, name="d_picked", offset=16384)
+        nc.vector.tensor_copy(out=d_picked[:], in_=d_word_tab[:].indirect(k1_sb[:]))
+        d_codes = keep.tile([P, H], U32, name="d_codes", align_bytes=64)
+        nc.vector.tensor_copy(out=d_codes[:].rearrange("p (t m) -> p m t", t=PACK), in_=d_picked[:].rearrange("p (m t) -> p m t", t=PACK))
+        x_codes = turns.tile([P, S], U32, name="x_codes", offset=20480, align_bytes=64)
+        nc.vector.tensor_copy(out=x_codes[:], in_=x_word_tab[:].indirect(offs_sb[:]))
+        d_plane = keep.tile([P, H], U8, name="d_plane", align_bytes=64)
+        nc.vector.tensor_copy(out=d_plane[:].rearrange("p (t m) -> p m t", t=PACK), in_=planes[:, S:].rearrange("p (m t) -> p m t", t=PACK))
+
+        twice = keep.tile([P, PACK], F32, name="twice")
+        sign = keep.tile([P, PACK], F32, name="sign")
+        sign_bf = keep.tile([P, PACK], BF16, name="sign_bf")
+        size = keep.tile([P, PACK], F32, name="size")
+        sixteenth = keep.tile([P, PACK], F32, name="sixteenth")
+        nc.gpsimd.tensor_scalar(out=twice[:], in0=gain[:], scalar1=0.0, scalar2=2.0, op0=ALU.is_ge, op1=ALU.mult)
+        nc.gpsimd.tensor_scalar(out=sign[:], in0=twice[:], scalar1=1.0, scalar2=-1.0, op0=ALU.mult, op1=ALU.add)
+        nc.gpsimd.tensor_scalar(out=sign_bf[:], in0=twice[:], scalar1=1.0, scalar2=-1.0, op0=ALU.mult, op1=ALU.add)
+        nc.gpsimd.tensor_scalar(out=sixteenth[:], in0=gain[:], scalar1=0.0625, scalar2=0.0, op0=ALU.mult, op1=ALU.add)
+        nc.gpsimd.tensor_tensor(out=size[:], in0=sixteenth[:], in1=sign[:], op=ALU.mult)
+
+        page = []
+        page_at = [0, 4096, 16384, 20480]
+        for m in range(3):
+            page.append(turns.tile([P, U], F32, name=f"page{m}", offset=page_at[m]))
+            nc.sync.dma_start(page[m][:], mem[m * P : (m + 1) * P, :])
+        w_raw = turns.tile([P, PACK, N], F32, name="w_raw", offset=8192)
+        nc.sync.dma_start(w_raw[:], w1.rearrange("(p t) n -> p t n", t=PACK))
+
+        h_bank = [psum.tile([P, S], F32, name=f"h_bank{t}") for t in range(PACK)]
+        for t in reversed(range(PACK)):
+            cols = slice(t * P, (t + 1) * P)
+            nc.tensor.matmul_mx(out=h_bank[t][:], lhsT=d_codes[:, cols].bitcast(FP8X4), lhsT_scale=d_plane[:, cols],
+                                rhs=x_codes[:].bitcast(FP8X4), rhs_scale=planes[:, :S], start=True, stop=True)
+        page.append(turns.tile([P, U], F32, name="page3", offset=page_at[3]))
+        nc.sync.dma_start(page[3][:], mem[3 * P : 4 * P, :])
+
+        gate = keep.tile([P, PACK * S], F32, name="gate")
+        gate_n1 = [keep.tile([P, S], F32, name=f"gate_n1_{t}") for t in range(PACK)]
+        st = keep.tile([P, PACK, S], F32, name="st")
+        st_flat = st[:].rearrange("p t j -> p (t j)")
+        st_n1 = keep.tile([P, PACK, S], F32, name="st_n1")
+        order = list(reversed(range(PACK)))
+        for t in order:
+            nc.scalar.activation(out=gate[:, t * S : (t + 1) * S], in_=h_bank[t][:], func=ACT.Sigmoid, scale=0.0625)
+        fetch(nc, True, gate_n1[0][:], gate[:, 0 : 2 * S].indirect(n1_sb[:]))
+        for t in order:
+            if t == PACK - 1:
+                for a in range(2):
+                    fetch(nc, False, gate_n1[t][:, half_cols(a)], gate[:, t * S : (t + 1) * S].indirect(half_list(n1_sb, a)))
+            elif t > 0:
+                fetch(nc, False, gate_n1[t][:], gate[:, t * S : (t + 2) * S].indirect(n1_sb[:]))
+            nc.vector.scalar_tensor_tensor(out=st[:, t, :], in0=h_bank[t][:], scalar=size[:, t : t + 1], in1=gate_n1[t][:],
+                                           op0=ALU.mult, op1=ALU.mult)
+            if t in (0, PACK - 1):
+                for a in range(2):
+                    fetch(nc, not (t == 0 and a == 0), st_n1[:, t, half_cols(a)], st[:, t, :].indirect(half_list(n1_sb, a)))
+            else:
+                fetch(nc, True, st_n1[:, t, :], st_flat[:, t * S : (t + 2) * S].indirect(n1_sb[:]))
+
+        z_size = keep.tile([P, S, PACK], BF16, name="z_size", align_bytes=64)
+        z_bf = keep.tile([P, S, PACK], BF16, name="z_bf", align_bytes=64)
+        z_codes = keep.tile([P, S], U32, name="z_codes", align_bytes=64)
+        z_plane = keep.tile([P, S], U8, name="z_plane", align_bytes=64)
+        for a in range(2):
+            js = half_cols(a)
+            nc.vector.tensor_tensor(out=z_size[:, js, :].rearrange("p (c i) t -> p c t i", i=4),
+                                    in0=st[:, :, js].rearrange("p t (c i) -> p c t i", i=4),
+                                    in1=st_n1[:, :, js].rearrange("p t (c i) -> p c t i", i=4), op=ALU.max)
+        for a in range(2):
+            js = half_cols(a)
+            nc.vector.tensor_tensor(out=z_bf[:, js, :], in0=z_size[:, js, :],
+                                    in1=sign_bf[:].rearrange("p (o t) -> p o t", o=1).to_broadcast([P, HALF, PACK]), op=ALU.mult)
+
+        w_bf = keep.tile([P, N, PACK], BF16, name="w_bf", align_bytes=64)
+        w_codes = keep.tile([P, N], U32, name="w_codes", align_bytes=64)
+        w_plane = keep.tile([P, N], U8, name="w_plane", align_bytes=64)
+        nc.vector.tensor_copy(out=w_bf[:].rearrange("p (c i) t -> p c t i", i=4), in_=w_raw[:].rearrange("p t (c i) -> p c t i", i=4))
+        for a in range(2):
+            js = half_cols(a)
+            nc.vector.quantize_mx(out=z_codes[:, js].bitcast(FP8X4), scales=z_plane[:, js], in_=z_bf[:, js, :].rearrange("p j t -> p (j t)"))
+        nc.vector.quantize_mx(out=w_codes[:].bitcast(FP8X4), scales=w_plane[:], in_=w_bf[:].rearrange("p n t -> p (n t)"))
+
+        old = [keep.tile([P, S], F32, name=f"old{m}") for m in range(4)]
+        for m in range(4):
+            fetch(nc, True, old[m][:], page[m][:].indirect(n2_sb[:]))
+
+        h2_bank = [psum.tile([P, S], F32, name=f"h2_bank{m}") for m in range(4)]
+        for m in range(4):
+            cols = slice(m * P, (m + 1) * P)
+            nc.tensor.matmul_mx(out=h2_bank[m][:], lhsT=w_codes[:, cols].bitcast(FP8X4), lhsT_scale=w_plane[:, cols],
+                                rhs=z_codes[:].bitcast(FP8X4), rhs_scale=z_plane[:], start=True, stop=True)
+        share = [keep.tile([P, S], F32, name=f"share{m}") for m in range(4)]
+        gap = [keep.tile([P, S], F32, name=f"gap{m}") for m in range(4)]
+        step = [keep.tile([P, S], F32, name=f"step{m}") for m in range(4)]
+        new = [keep.tile([P, S], F32, name=f"new{m}") for m in range(3)]
+        for m in range(4):
+            nc.scalar.activation(out=share[m][:], in_=h2_bank[m][:], func=ACT.Sigmoid)
+        on_scalar = {0: (0, 1), 1: (0, 1), 2: (1,), 3: ()}
+        for m in range(5):
+            if m < 4:
+                nc.vector.tensor_tensor(out=gap[m][:], in0=h2_bank[m][:], in1=old[m][:], op=ALU.subtract)
+            if m > 0 and on_scalar[m - 1]:
+                js = slice(on_scalar[m - 1][0] * HALF, S)
+                nc.vector.tensor_tensor(out=new[m - 1][:, js], in0=step[m - 1][:, js], in1=old[m - 1][:, js], op=ALU.add)
+            if m < 4:
+                nc.vector.tensor_tensor(out=step[m][:], in0=gap[m][:], in1=share[m][:], op=ALU.mult)
+        for m in range(4):
+            if not on_scalar[m]:
+                nc.vector.tensor_tensor(out=page[m][:].indirect(n2_sb[:]), in0=step[m][:], in1=old[m][:], op=ALU.add)
+            else:
+                for a in range(2):
+                    js = half_cols(a)
+                    if a in on_scalar[m]:
+                        nc.scalar.activation(out=page[m][:].indirect(half_list(n2_sb, a)), in_=new[m][:, js], func=ACT.Copy)
+                    else:
+                        nc.vector.tensor_tensor(out=page[m][:].indirect(half_list(n2_sb, a)), in0=step[m][:, js], in1=old[m][:, js], op=ALU.add)
+            nc.sync.dma_start(out[m * P : (m + 1) * P, :], page[m][:])

@@ -17,6 +17,9 @@ PACK = 4
 K, T, S, N, G, H, U = 512, 2048, 512, 512, 2048, 512, 1024
 HALF = S // 2
 LIST_COLS = S // 16
+SPARE = 16
+SCALAR_TAIL = 192
+AT_D, AT_PICKED, AT_BYTES, AT_X, AT_GATE, AT_Z = 0, 8192, 12288, 16384, 32768, 49152
 FLOPS = 2 * K * H * S + 2 * H * N * S
 
 
@@ -50,37 +53,44 @@ def tile_picked_hpqtwicppaget_none_p_kernel(tc, x_words, x_scales, d_words, d_sc
         x_scale_tab = keep.tile([P, T], U8, name="x_scale_tab", align_bytes=64)
         d_scale_tab = keep.tile([P, G], U8, name="d_scale_tab", align_bytes=64)
         planes = keep.tile([P, S + H], U8, name="planes", align_bytes=64)
-        nc.vector.memset(x_scale_tab[:].bitcast(I32), 0)
         nc.vector.memset(d_scale_tab[:].bitcast(I32), 0)
+        nc.vector.memset(x_scale_tab[:].bitcast(I32), 0)
         nc.vector.memset(planes[:].bitcast(I32), 0)
 
-        nc.sync.dma_start(offs_sb[:], offs)
+        d_word_tab = turns.tile([P, G], U32, name="d_word_tab", offset=AT_D)
+        x_word_tab = turns.tile([P, T], U32, name="x_word_tab", offset=AT_X)
+        d_rows = d_words[0].rearrange("p n t -> p (n t)").bitcast(I32)
         nc.sync.dma_start(k1_sb[:], k1)
+        nc.sync.dma_start(offs_sb[:], offs)
+        nc.sync.dma_start(d_word_tab[:, : G // 2].bitcast(I32), d_rows[:, : G // 2])
+        nc.sync.dma_start(d_scale_tab[0:P:8, :].bitcast(I32), d_scales[0].bitcast(I32))
+        nc.sync.dma_start(x_scale_tab[0:P:8, :].bitcast(I32), x_scales[0].bitcast(I32))
         nc.sync.dma_start(n1_sb[:], n1)
         nc.sync.dma_start(n2_sb[:], n2)
-        gain = keep.tile([P, PACK], F32, name="gain")
-        nc.sync.dma_start(gain[:], gn.rearrange("(p t) o -> p (t o)", t=PACK))
-        nc.sync.dma_start(x_scale_tab[0:P:8, :].bitcast(I32), x_scales[0].bitcast(I32))
-        nc.sync.dma_start(d_scale_tab[0:P:8, :].bitcast(I32), d_scales[0].bitcast(I32))
-        d_word_tab = turns.tile([P, G], U32, name="d_word_tab", offset=0)
-        x_word_tab = turns.tile([P, T], U32, name="x_word_tab", offset=8192)
-        nc.sync.dma_start(d_word_tab[:].bitcast(I32), d_words[0].rearrange("p n t -> p (n t)").bitcast(I32))
+        nc.sync.dma_start(d_word_tab[:, G // 2 :].bitcast(I32), d_rows[:, G // 2 :])
+        w_rows = w1.rearrange("(p t) n -> p t n", t=PACK)
+        w_raw = [keep.tile([P, PACK, N // 2], F32, name=f"w_raw{a}") for a in range(2)]
+        nc.sync.dma_start(w_raw[0][:], w_rows[:, :, : N // 2])
         nc.sync.dma_start(x_word_tab[:].bitcast(I32), x_words[0].rearrange("p n t -> p (n t)").bitcast(I32))
+        nc.sync.dma_start(w_raw[1][:], w_rows[:, :, N // 2 :])
+        gain = keep.tile([P, PACK], F32, name="gain")
+        nc.gpsimd.dma_start(gain[:], gn.rearrange("(p t) o -> p (t o)", t=PACK))
 
-        picked_bytes = keep.tile([P, S + H], U8, name="picked_bytes", align_bytes=64)
-        nc.vector.tensor_copy(out=picked_bytes[:, :S], in_=x_scale_tab[:].indirect(offs_sb[:]))
+        picked_bytes = turns.tile([P, S + H], U8, name="picked_bytes", align_bytes=64, offset=AT_PICKED)
+        dealt_bytes = turns.tile([P, S + H], U8, name="dealt_bytes", align_bytes=64, offset=AT_BYTES)
         nc.vector.tensor_copy(out=picked_bytes[:, S:], in_=d_scale_tab[:].indirect(k1_sb[:]))
+        nc.vector.tensor_copy(out=picked_bytes[:, :S], in_=x_scale_tab[:].indirect(offs_sb[:]))
+        nc.vector.tensor_copy(out=dealt_bytes[:, S:].rearrange("p (t m) -> p m t", t=PACK), in_=picked_bytes[:, S:].rearrange("p (m t) -> p m t", t=PACK))
+        nc.vector.tensor_copy(out=dealt_bytes[:, :S].bitcast(I32), in_=picked_bytes[:, :S].bitcast(I32))
         for r in range(4):
-            nc.scalar.dma_start(planes[r:P:32, :].bitcast(I32), picked_bytes[8 * r : P : 32, :].bitcast(I32))
+            nc.scalar.dma_start(planes[r:P:32, :].bitcast(I32), dealt_bytes[8 * r : P : 32, :].bitcast(I32))
 
-        d_picked = turns.tile([P, H], U32, name="d_picked", offset=16384)
+        d_picked = turns.tile([P, H], U32, name="d_picked", offset=AT_PICKED)
         nc.vector.tensor_copy(out=d_picked[:], in_=d_word_tab[:].indirect(k1_sb[:]))
         d_codes = keep.tile([P, H], U32, name="d_codes", align_bytes=64)
         nc.vector.tensor_copy(out=d_codes[:].rearrange("p (t m) -> p m t", t=PACK), in_=d_picked[:].rearrange("p (m t) -> p m t", t=PACK))
-        x_codes = turns.tile([P, S], U32, name="x_codes", offset=20480, align_bytes=64)
+        x_codes = keep.tile([P, S], U32, name="x_codes", align_bytes=64)
         nc.vector.tensor_copy(out=x_codes[:], in_=x_word_tab[:].indirect(offs_sb[:]))
-        d_plane = keep.tile([P, H], U8, name="d_plane", align_bytes=64)
-        nc.vector.tensor_copy(out=d_plane[:].rearrange("p (t m) -> p m t", t=PACK), in_=planes[:, S:].rearrange("p (m t) -> p m t", t=PACK))
 
         twice = keep.tile([P, PACK], F32, name="twice")
         sign = keep.tile([P, PACK], F32, name="sign")
@@ -93,100 +103,87 @@ def tile_picked_hpqtwicppaget_none_p_kernel(tc, x_words, x_scales, d_words, d_sc
         nc.gpsimd.tensor_scalar(out=sixteenth[:], in0=gain[:], scalar1=0.0625, scalar2=0.0, op0=ALU.mult, op1=ALU.add)
         nc.gpsimd.tensor_tensor(out=size[:], in0=sixteenth[:], in1=sign[:], op=ALU.mult)
 
-        page = []
-        page_at = [0, 4096, 16384, 20480]
-        for m in range(3):
-            page.append(turns.tile([P, U], F32, name=f"page{m}", offset=page_at[m]))
+        page = {}
+        for m, at in enumerate((AT_D, AT_D + 4096, AT_PICKED, AT_BYTES)):
+            page[m] = turns.tile([P, U], F32, name=f"page{m}", offset=at)
             nc.sync.dma_start(page[m][:], mem[m * P : (m + 1) * P, :])
-        w_raw = turns.tile([P, PACK, N], F32, name="w_raw", offset=8192)
-        nc.sync.dma_start(w_raw[:], w1.rearrange("(p t) n -> p t n", t=PACK))
+
+        w_codes = turns.tile([P, N], U32, name="w_codes", align_bytes=64, offset=AT_X + 2048)
+        w_plane = keep.tile([P, N], U8, name="w_plane", align_bytes=64)
+        w_bf = [keep.tile([P, N // 2, PACK], BF16, name="w_bf0", align_bytes=64),
+                turns.tile([P, N // 2, PACK], BF16, name="w_bf1", align_bytes=64, offset=AT_X)]
+        for a, cast in enumerate((nc.scalar.copy, nc.vector.tensor_copy)):
+            cast(out=w_bf[a][:].rearrange("p (c i) t -> p c t i", i=4), in_=w_raw[a][:].rearrange("p t (c i) -> p c t i", i=4))
+        for a in range(2):
+            ns = slice(a * N // 2, (a + 1) * N // 2)
+            nc.vector.quantize_mx(out=w_codes[:, ns].bitcast(FP8X4), scales=w_plane[:, ns], in_=w_bf[a][:].rearrange("p n t -> p (n t)"))
 
         h_bank = [psum.tile([P, S], F32, name=f"h_bank{t}") for t in range(PACK)]
-        for t in reversed(range(PACK)):
+        for t in range(PACK):
             cols = slice(t * P, (t + 1) * P)
-            nc.tensor.matmul_mx(out=h_bank[t][:], lhsT=d_codes[:, cols].bitcast(FP8X4), lhsT_scale=d_plane[:, cols],
+            nc.tensor.matmul_mx(out=h_bank[t][:], lhsT=d_codes[:, cols].bitcast(FP8X4), lhsT_scale=planes[:, S + t * P : S + (t + 1) * P],
                                 rhs=x_codes[:].bitcast(FP8X4), rhs_scale=planes[:, :S], start=True, stop=True)
-        page.append(turns.tile([P, U], F32, name="page3", offset=page_at[3]))
-        nc.sync.dma_start(page[3][:], mem[3 * P : 4 * P, :])
 
-        gate = keep.tile([P, PACK * S], F32, name="gate")
-        gate_n1 = [keep.tile([P, S], F32, name=f"gate_n1_{t}") for t in range(PACK)]
+        gate = [turns.tile([P, S + SPARE], F32, name=f"gate{t}", offset=AT_GATE + 4 * (S + SPARE) * (PACK - 1 - t)) for t in range(PACK)]
+        for t in range(PACK):
+            nc.gpsimd.memset(gate[t][:, S:], 0.0)
+        h_sized = [keep.tile([P, S], F32, name=f"h_sized{t}") for t in range(PACK)]
         st = keep.tile([P, PACK, S], F32, name="st")
-        st_flat = st[:].rearrange("p t j -> p (t j)")
         st_n1 = keep.tile([P, PACK, S], F32, name="st_n1")
-        order = list(reversed(range(PACK)))
-        for t in order:
-            nc.scalar.activation(out=gate[:, t * S : (t + 1) * S], in_=h_bank[t][:], func=ACT.Sigmoid, scale=0.0625)
-        fetch(nc, True, gate_n1[0][:], gate[:, 0 : 2 * S].indirect(n1_sb[:]))
-        for t in order:
-            if t == PACK - 1:
-                for a in range(2):
-                    fetch(nc, False, gate_n1[t][:, half_cols(a)], gate[:, t * S : (t + 1) * S].indirect(half_list(n1_sb, a)))
-            elif t > 0:
-                fetch(nc, False, gate_n1[t][:], gate[:, t * S : (t + 2) * S].indirect(n1_sb[:]))
-            nc.vector.scalar_tensor_tensor(out=st[:, t, :], in0=h_bank[t][:], scalar=size[:, t : t + 1], in1=gate_n1[t][:],
-                                           op0=ALU.mult, op1=ALU.mult)
-            if t in (0, PACK - 1):
-                for a in range(2):
-                    fetch(nc, not (t == 0 and a == 0), st_n1[:, t, half_cols(a)], st[:, t, :].indirect(half_list(n1_sb, a)))
-            else:
-                fetch(nc, True, st_n1[:, t, :], st_flat[:, t * S : (t + 2) * S].indirect(n1_sb[:]))
+        for t in range(PACK):
+            nc.scalar.activation(out=gate[t][:, :S], in_=h_bank[t][:], func=ACT.Sigmoid, scale=0.0625)
+            nc.scalar.activation(out=h_sized[t][:], in_=h_bank[t][:], func=ACT.Copy, scale=size[:, t : t + 1])
+        for t in range(PACK):
+            nc.vector.tensor_tensor(out=st[:, t, :], in0=gate[t][:].indirect(n1_sb[:]), in1=h_sized[t][:], op=ALU.mult)
+        for a in range(2):
+            for t in range(PACK):
+                fetch(nc, (t, a) != (PACK - 1, 0), st_n1[:, t, half_cols(a)], st[:, t, :].indirect(half_list(n1_sb, a)))
 
-        z_size = keep.tile([P, S, PACK], BF16, name="z_size", align_bytes=64)
-        z_bf = keep.tile([P, S, PACK], BF16, name="z_bf", align_bytes=64)
         z_codes = keep.tile([P, S], U32, name="z_codes", align_bytes=64)
         z_plane = keep.tile([P, S], U8, name="z_plane", align_bytes=64)
+        old = [turns.tile([P, 2, S], F32, name="old0", offset=AT_GATE - 4096 + 64)]
+        for m in range(2):
+            fetch(nc, True, old[m // 2][:, m % 2, :], page[m][:].indirect(n2_sb[:]))
+        h2_bank = [[psum.tile([P, 2, HALF], F32, name=f"h2_bank{a}{b}") for b in range(2)] for a in range(2)]
+        share = keep.tile([P, 4, S], F32, name="share")
+        gap = keep.tile([P, 4, S], F32, name="gap")
+        step = keep.tile([P, 4, S], F32, name="step")
+        new = keep.tile([P, 3, S], F32, name="new")
         for a in range(2):
             js = half_cols(a)
-            nc.vector.tensor_tensor(out=z_size[:, js, :].rearrange("p (c i) t -> p c t i", i=4),
+            z_size = keep.tile([P, HALF, PACK], BF16, name="z_size", align_bytes=64)
+            nc.vector.tensor_tensor(out=z_size[:].rearrange("p (c i) t -> p c t i", i=4),
                                     in0=st[:, :, js].rearrange("p t (c i) -> p c t i", i=4),
                                     in1=st_n1[:, :, js].rearrange("p t (c i) -> p c t i", i=4), op=ALU.max)
-        for a in range(2):
-            js = half_cols(a)
-            nc.vector.tensor_tensor(out=z_bf[:, js, :], in0=z_size[:, js, :],
+            z_bf = turns.tile([P, HALF, PACK], BF16, name=f"z_bf{a}", align_bytes=64, offset=AT_Z + 4096 * a)
+            nc.vector.tensor_tensor(out=z_bf[:], in0=z_size[:],
                                     in1=sign_bf[:].rearrange("p (o t) -> p o t", o=1).to_broadcast([P, HALF, PACK]), op=ALU.mult)
-
-        w_bf = keep.tile([P, N, PACK], BF16, name="w_bf", align_bytes=64)
-        w_codes = keep.tile([P, N], U32, name="w_codes", align_bytes=64)
-        w_plane = keep.tile([P, N], U8, name="w_plane", align_bytes=64)
-        nc.vector.tensor_copy(out=w_bf[:].rearrange("p (c i) t -> p c t i", i=4), in_=w_raw[:].rearrange("p t (c i) -> p c t i", i=4))
-        for a in range(2):
-            js = half_cols(a)
-            nc.vector.quantize_mx(out=z_codes[:, js].bitcast(FP8X4), scales=z_plane[:, js], in_=z_bf[:, js, :].rearrange("p j t -> p (j t)"))
-        nc.vector.quantize_mx(out=w_codes[:].bitcast(FP8X4), scales=w_plane[:], in_=w_bf[:].rearrange("p n t -> p (n t)"))
-
-        old = [keep.tile([P, S], F32, name=f"old{m}") for m in range(4)]
-        for m in range(4):
-            fetch(nc, True, old[m][:], page[m][:].indirect(n2_sb[:]))
-
-        h2_bank = [psum.tile([P, S], F32, name=f"h2_bank{m}") for m in range(4)]
-        for m in range(4):
-            cols = slice(m * P, (m + 1) * P)
-            nc.tensor.matmul_mx(out=h2_bank[m][:], lhsT=w_codes[:, cols].bitcast(FP8X4), lhsT_scale=w_plane[:, cols],
-                                rhs=z_codes[:].bitcast(FP8X4), rhs_scale=z_plane[:], start=True, stop=True)
-        share = [keep.tile([P, S], F32, name=f"share{m}") for m in range(4)]
-        gap = [keep.tile([P, S], F32, name=f"gap{m}") for m in range(4)]
-        step = [keep.tile([P, S], F32, name=f"step{m}") for m in range(4)]
-        new = [keep.tile([P, S], F32, name=f"new{m}") for m in range(3)]
-        for m in range(4):
-            nc.scalar.activation(out=share[m][:], in_=h2_bank[m][:], func=ACT.Sigmoid)
-        on_scalar = {0: (0, 1), 1: (0, 1), 2: (1,), 3: ()}
-        for m in range(5):
-            if m < 4:
-                nc.vector.tensor_tensor(out=gap[m][:], in0=h2_bank[m][:], in1=old[m][:], op=ALU.subtract)
-            if m > 0 and on_scalar[m - 1]:
-                js = slice(on_scalar[m - 1][0] * HALF, S)
-                nc.vector.tensor_tensor(out=new[m - 1][:, js], in0=step[m - 1][:, js], in1=old[m - 1][:, js], op=ALU.add)
-            if m < 4:
-                nc.vector.tensor_tensor(out=step[m][:], in0=gap[m][:], in1=share[m][:], op=ALU.mult)
-        for m in range(4):
-            if not on_scalar[m]:
-                nc.vector.tensor_tensor(out=page[m][:].indirect(n2_sb[:]), in0=step[m][:], in1=old[m][:], op=ALU.add)
-            else:
-                for a in range(2):
-                    js = half_cols(a)
-                    if a in on_scalar[m]:
-                        nc.scalar.activation(out=page[m][:].indirect(half_list(n2_sb, a)), in_=new[m][:, js], func=ACT.Copy)
-                    else:
-                        nc.vector.tensor_tensor(out=page[m][:].indirect(half_list(n2_sb, a)), in0=step[m][:, js], in1=old[m][:, js], op=ALU.add)
+            nc.vector.quantize_mx(out=z_codes[:, js].bitcast(FP8X4), scales=z_plane[:, js], in_=z_bf[:].rearrange("p j t -> p (j t)"))
+            for m in range(4):
+                cols = slice(m * P, (m + 1) * P)
+                nc.tensor.matmul_mx(out=h2_bank[a][m // 2][:, m % 2, :], lhsT=w_codes[:, cols].bitcast(FP8X4), lhsT_scale=w_plane[:, cols],
+                                    rhs=z_codes[:, js].bitcast(FP8X4), rhs_scale=z_plane[:, js], start=True, stop=True)
+            for b in range(2):
+                nc.scalar.activation(out=share[:, 2 * b : 2 * b + 2, js], in_=h2_bank[a][b][:], func=ACT.Sigmoid)
+        old.append(turns.tile([P, 2, S], F32, name="old1", offset=AT_Z))
+        for m in range(2, 4):
+            fetch(nc, True, old[1][:, m % 2, :], page[m][:].indirect(n2_sb[:]))
+        for b in range(2):
+            ms = slice(2 * b, 2 * b + 2)
+            for a in range(2):
+                js = half_cols(a)
+                nc.vector.tensor_tensor(out=gap[:, ms, js], in0=h2_bank[a][b][:], in1=old[b][:, :, js], op=ALU.subtract)
+                nc.vector.tensor_tensor(out=step[:, ms, js], in0=gap[:, ms, js], in1=share[:, ms, js], op=ALU.mult)
+                if b == 0:
+                    nc.vector.tensor_tensor(out=new[:, ms, js], in0=step[:, ms, js], in1=old[b][:, :, js], op=ALU.add)
+        cut = S - SCALAR_TAIL
+        nc.vector.tensor_tensor(out=new[:, 2, cut:], in0=step[:, 2, cut:], in1=old[1][:, 0, cut:], op=ALU.add)
+        for m in range(2):
+            for a in range(2):
+                nc.scalar.activation(out=page[m][:].indirect(half_list(n2_sb, a)), in_=new[:, m, half_cols(a)], func=ACT.Copy)
+            nc.sync.dma_start(out[m * P : (m + 1) * P, :], page[m][:])
+        nc.vector.tensor_tensor(out=page[2][:].indirect(n2_sb[:, : cut // 16]), in0=step[:, 2, :cut], in1=old[1][:, 0, :cut], op=ALU.add)
+        nc.vector.tensor_tensor(out=page[3][:].indirect(n2_sb[:]), in0=step[:, 3, :], in1=old[1][:, 1, :], op=ALU.add)
+        nc.scalar.activation(out=page[2][:].indirect(n2_sb[:, cut // 16 :]), in_=new[:, 2, cut:], func=ACT.Copy)
+        for m in range(2, 4):
             nc.sync.dma_start(out[m * P : (m + 1) * P, :], page[m][:])

@@ -80,15 +80,15 @@ def tile_picked_hpqtwicppaget_none_p_kernel(tc, x_words, x_scales, d_words, d_sc
         dealt_bytes = turns.tile([P, S + H], U8, name="dealt_bytes", align_bytes=64, offset=AT_BYTES)
         nc.vector.tensor_copy(out=picked_bytes[:, S:], in_=d_scale_tab[:].indirect(k1_sb[:]))
         nc.vector.tensor_copy(out=picked_bytes[:, :S], in_=x_scale_tab[:].indirect(offs_sb[:]))
-        nc.vector.tensor_copy(out=dealt_bytes[:, S:].rearrange("p (t m) -> p m t", t=PACK), in_=picked_bytes[:, S:].rearrange("p (m t) -> p m t", t=PACK))
+        nc.vector.tensor_copy(out=dealt_bytes[:, S:].rearrange("p (t m) -> p t m", t=PACK), in_=picked_bytes[:, S:].rearrange("p (m t) -> p t m", t=PACK))
         nc.vector.tensor_copy(out=dealt_bytes[:, :S].bitcast(I32), in_=picked_bytes[:, :S].bitcast(I32))
         for r in range(4):
-            nc.scalar.dma_start(planes[r:P:32, :].bitcast(I32), dealt_bytes[8 * r : P : 32, :].bitcast(I32))
+            nc.sync.dma_start(planes[r:P:32, :].bitcast(I32), dealt_bytes[8 * r : P : 32, :].bitcast(I32))
 
         d_picked = turns.tile([P, H], U32, name="d_picked", offset=AT_PICKED)
         nc.vector.tensor_copy(out=d_picked[:], in_=d_word_tab[:].indirect(k1_sb[:]))
         d_codes = keep.tile([P, H], U32, name="d_codes", align_bytes=64)
-        nc.vector.tensor_copy(out=d_codes[:].rearrange("p (t m) -> p m t", t=PACK), in_=d_picked[:].rearrange("p (m t) -> p m t", t=PACK))
+        nc.vector.tensor_copy(out=d_codes[:].rearrange("p (t c i) -> p c t i", t=PACK, i=4), in_=d_picked[:].rearrange("p (c i t) -> p c t i", t=PACK, i=4))
         x_codes = keep.tile([P, S], U32, name="x_codes", align_bytes=64)
         nc.vector.tensor_copy(out=x_codes[:], in_=x_word_tab[:].indirect(offs_sb[:]))
 
@@ -152,9 +152,9 @@ def tile_picked_hpqtwicppaget_none_p_kernel(tc, x_words, x_scales, d_words, d_sc
         for a in range(2):
             js = half_cols(a)
             z_size = keep.tile([P, HALF, PACK], BF16, name="z_size", align_bytes=64)
-            nc.vector.tensor_tensor(out=z_size[:].rearrange("p (c i) t -> p c t i", i=4),
-                                    in0=st[:, :, js].rearrange("p t (c i) -> p c t i", i=4),
-                                    in1=st_n1[:, :, js].rearrange("p t (c i) -> p c t i", i=4), op=ALU.max)
+            nc.vector.tensor_tensor(out=z_size[:].rearrange("p (c i) t -> p c t i", i=2),
+                                    in0=st[:, :, js].rearrange("p t (c i) -> p c t i", i=2),
+                                    in1=st_n1[:, :, js].rearrange("p t (c i) -> p c t i", i=2), op=ALU.max)
             z_bf = turns.tile([P, HALF, PACK], BF16, name=f"z_bf{a}", align_bytes=64, offset=AT_Z + 4096 * a)
             nc.vector.tensor_tensor(out=z_bf[:], in0=z_size[:],
                                     in1=sign_bf[:].rearrange("p (o t) -> p o t", o=1).to_broadcast([P, HALF, PACK]), op=ALU.mult)

@@ -62,16 +62,15 @@ def tile_picked_hpqtwicppaget_none_p_kernel(tc, x_words, x_scales, d_words, d_sc
         d_rows = d_words[0].rearrange("p n t -> p (n t)").bitcast(I32)
         nc.sync.dma_start(k1_sb[:], k1)
         nc.sync.dma_start(offs_sb[:], offs)
-        nc.sync.dma_start(d_word_tab[:, : G // 2].bitcast(I32), d_rows[:, : G // 2])
         nc.sync.dma_start(d_scale_tab[0:P:8, :].bitcast(I32), d_scales[0].bitcast(I32))
         nc.sync.dma_start(x_scale_tab[0:P:8, :].bitcast(I32), x_scales[0].bitcast(I32))
         nc.sync.dma_start(n1_sb[:], n1)
         nc.sync.dma_start(n2_sb[:], n2)
-        nc.sync.dma_start(d_word_tab[:, G // 2 :].bitcast(I32), d_rows[:, G // 2 :])
+        nc.sync.dma_start(d_word_tab[:].bitcast(I32), d_rows)
         w_rows = w1.rearrange("(p t) n -> p t n", t=PACK)
         w_raw = [keep.tile([P, PACK, N // 2], F32, name=f"w_raw{a}") for a in range(2)]
-        nc.sync.dma_start(w_raw[0][:], w_rows[:, :, : N // 2])
         nc.sync.dma_start(x_word_tab[:].bitcast(I32), x_words[0].rearrange("p n t -> p (n t)").bitcast(I32))
+        nc.sync.dma_start(w_raw[0][:], w_rows[:, :, : N // 2])
         nc.sync.dma_start(w_raw[1][:], w_rows[:, :, N // 2 :])
         gain = keep.tile([P, PACK], F32, name="gain")
         nc.gpsimd.dma_start(gain[:], gn.rearrange("(p t) o -> p (t o)", t=PACK))
@@ -83,7 +82,7 @@ def tile_picked_hpqtwicppaget_none_p_kernel(tc, x_words, x_scales, d_words, d_sc
         nc.vector.tensor_copy(out=dealt_bytes[:, S:].rearrange("p (t m) -> p t m", t=PACK), in_=picked_bytes[:, S:].rearrange("p (m t) -> p t m", t=PACK))
         nc.vector.tensor_copy(out=dealt_bytes[:, :S].bitcast(I32), in_=picked_bytes[:, :S].bitcast(I32))
         for r in range(4):
-            nc.sync.dma_start(planes[r:P:32, :].bitcast(I32), dealt_bytes[8 * r : P : 32, :].bitcast(I32))
+            nc.scalar.dma_start(planes[r:P:32, :].bitcast(I32), dealt_bytes[8 * r : P : 32, :].bitcast(I32))
 
         d_picked = turns.tile([P, H], U32, name="d_picked", offset=AT_PICKED)
         nc.vector.tensor_copy(out=d_picked[:], in_=d_word_tab[:].indirect(k1_sb[:]))
@@ -108,12 +107,11 @@ def tile_picked_hpqtwicppaget_none_p_kernel(tc, x_words, x_scales, d_words, d_sc
             page[m] = turns.tile([P, U], F32, name=f"page{m}", offset=at)
             nc.sync.dma_start(page[m][:], mem[m * P : (m + 1) * P, :])
 
-        w_codes = turns.tile([P, N], U32, name="w_codes", align_bytes=64, offset=AT_X + 2048)
+        w_codes = keep.tile([P, N], U32, name="w_codes", align_bytes=64)
         w_plane = keep.tile([P, N], U8, name="w_plane", align_bytes=64)
-        w_bf = [keep.tile([P, N // 2, PACK], BF16, name="w_bf0", align_bytes=64),
-                turns.tile([P, N // 2, PACK], BF16, name="w_bf1", align_bytes=64, offset=AT_X)]
-        for a, cast in enumerate((nc.scalar.copy, nc.vector.tensor_copy)):
-            cast(out=w_bf[a][:].rearrange("p (c i) t -> p c t i", i=4), in_=w_raw[a][:].rearrange("p t (c i) -> p c t i", i=4))
+        w_bf = [turns.tile([P, N // 2, PACK], BF16, name=f"w_bf{a}", align_bytes=64, offset=AT_X + 2048 * a) for a in range(2)]
+        for a in range(2):
+            nc.vector.tensor_copy(out=w_bf[a][:].rearrange("p (c i) t -> p c t i", i=4), in_=w_raw[a][:].rearrange("p t (c i) -> p c t i", i=4))
         for a in range(2):
             ns = slice(a * N // 2, (a + 1) * N // 2)
             nc.vector.quantize_mx(out=w_codes[:, ns].bitcast(FP8X4), scales=w_plane[:, ns], in_=w_bf[a][:].rearrange("p n t -> p (n t)"))

@@ -14,13 +14,24 @@ ACT = mybir.ActivationFunctionType
 
 P = 128
 PACK = 4
+PAGES = 4
 K, T, S, N, G, H, U = 512, 2048, 512, 512, 2048, 512, 1024
 HALF = S // 2
 LIST_COLS = S // 16
+ALPHA = 0.0625
 SPARE = 16
 SCALAR_TAIL = 192
-AT_D, AT_PICKED, AT_BYTES, AT_X, AT_GATE, AT_Z = 0, 8192, 12288, 16384, 32768, 49152
 FLOPS = 2 * K * H * S + 2 * H * N * S
+
+TILE_BYTES = 4 * S
+PAGE_BYTES = 4 * U
+AT_D = 0
+AT_PICKED = 2 * PAGE_BYTES
+AT_DEALT = 3 * PAGE_BYTES
+AT_X = 4 * PAGE_BYTES
+AT_GATE = 8 * PAGE_BYTES
+AT_OLD_01 = AT_GATE - PAGE_BYTES + 64
+AT_Z = 12 * PAGE_BYTES
 
 
 def half_cols(a):
@@ -31,14 +42,13 @@ def half_list(lst, a):
     return lst[:, a * LIST_COLS // 2 : (a + 1) * LIST_COLS // 2]
 
 
-def fetch(nc, on_scalar, out, window):
-    if on_scalar:
-        nc.scalar.activation(out=out, in_=window, func=ACT.Copy)
-    else:
-        nc.vector.tensor_copy(out=out, in_=window)
+def scalar_move(nc, out, in_):
+    nc.scalar.activation(out=out, in_=in_, func=ACT.Copy)
 
 
-def tile_picked_hpqtwicppaget_none_p_kernel(tc, x_words, x_scales, d_words, d_scales, gn, w1, mem, offs, k1, n1, n2, out):
+def tile_picked_hpqtwicppaget_none_p_kernel(
+    tc, x_words, x_scales, d_words, d_scales, gn, w1, mem, offs, k1, n1, n2, out
+):
     nc = tc.nc
     with ExitStack() as ctx:
         keep = ctx.enter_context(tc.tile_pool(name="keep", bufs=1))
@@ -59,113 +69,159 @@ def tile_picked_hpqtwicppaget_none_p_kernel(tc, x_words, x_scales, d_words, d_sc
 
         d_word_tab = turns.tile([P, G], U32, name="d_word_tab", offset=AT_D)
         x_word_tab = turns.tile([P, T], U32, name="x_word_tab", offset=AT_X)
-        d_rows = d_words[0].rearrange("p n t -> p (n t)").bitcast(I32)
         nc.sync.dma_start(k1_sb[:], k1)
         nc.sync.dma_start(offs_sb[:], offs)
         nc.sync.dma_start(d_scale_tab[0:P:8, :].bitcast(I32), d_scales[0].bitcast(I32))
         nc.sync.dma_start(x_scale_tab[0:P:8, :].bitcast(I32), x_scales[0].bitcast(I32))
         nc.sync.dma_start(n1_sb[:], n1)
         nc.sync.dma_start(n2_sb[:], n2)
-        nc.sync.dma_start(d_word_tab[:].bitcast(I32), d_rows)
-        w_rows = w1.rearrange("(p t) n -> p t n", t=PACK)
-        w_raw = [keep.tile([P, PACK, N // 2], F32, name=f"w_raw{a}") for a in range(2)]
+        nc.sync.dma_start(d_word_tab[:].bitcast(I32), d_words[0].rearrange("p n t -> p (n t)").bitcast(I32))
         nc.sync.dma_start(x_word_tab[:].bitcast(I32), x_words[0].rearrange("p n t -> p (n t)").bitcast(I32))
+        w_rows = w1.rearrange("(p t) n -> p t n", t=PACK)
+        w_raw = [keep.tile([P, PACK, N // 2], F32, name="w_raw0")]
         nc.sync.dma_start(w_raw[0][:], w_rows[:, :, : N // 2])
-        nc.sync.dma_start(w_raw[1][:], w_rows[:, :, N // 2 :])
         gain = keep.tile([P, PACK], F32, name="gain")
         nc.gpsimd.dma_start(gain[:], gn.rearrange("(p t) o -> p (t o)", t=PACK))
 
         picked_bytes = turns.tile([P, S + H], U8, name="picked_bytes", align_bytes=64, offset=AT_PICKED)
-        dealt_bytes = turns.tile([P, S + H], U8, name="dealt_bytes", align_bytes=64, offset=AT_BYTES)
+        dealt_bytes = turns.tile([P, S + H], U8, name="dealt_bytes", align_bytes=64, offset=AT_DEALT)
         nc.vector.tensor_copy(out=picked_bytes[:, S:], in_=d_scale_tab[:].indirect(k1_sb[:]))
         nc.vector.tensor_copy(out=picked_bytes[:, :S], in_=x_scale_tab[:].indirect(offs_sb[:]))
-        nc.vector.tensor_copy(out=dealt_bytes[:, S:].rearrange("p (t m) -> p t m", t=PACK), in_=picked_bytes[:, S:].rearrange("p (m t) -> p t m", t=PACK))
+        nc.vector.tensor_copy(
+            out=dealt_bytes[:, S:].rearrange("p (t c) -> p t c", t=PACK),
+            in_=picked_bytes[:, S:].rearrange("p (c t) -> p t c", t=PACK),
+        )
         nc.vector.tensor_copy(out=dealt_bytes[:, :S].bitcast(I32), in_=picked_bytes[:, :S].bitcast(I32))
         for r in range(4):
-            nc.scalar.dma_start(planes[r:P:32, :].bitcast(I32), dealt_bytes[8 * r : P : 32, :].bitcast(I32))
+            nc.sync.dma_start(planes[r:P:32, :].bitcast(I32), dealt_bytes[8 * r : P : 32, :].bitcast(I32))
 
         d_picked = turns.tile([P, H], U32, name="d_picked", offset=AT_PICKED)
         nc.vector.tensor_copy(out=d_picked[:], in_=d_word_tab[:].indirect(k1_sb[:]))
         d_codes = keep.tile([P, H], U32, name="d_codes", align_bytes=64)
-        nc.vector.tensor_copy(out=d_codes[:].rearrange("p (t c i) -> p c t i", t=PACK, i=4), in_=d_picked[:].rearrange("p (c i t) -> p c t i", t=PACK, i=4))
+        nc.vector.tensor_copy(
+            out=d_codes[:].rearrange("p (t c e) -> p c t e", t=PACK, e=4),
+            in_=d_picked[:].rearrange("p (c e t) -> p c t e", t=PACK, e=4),
+        )
         x_codes = keep.tile([P, S], U32, name="x_codes", align_bytes=64)
         nc.vector.tensor_copy(out=x_codes[:], in_=x_word_tab[:].indirect(offs_sb[:]))
 
-        twice = keep.tile([P, PACK], F32, name="twice")
+        two_if_positive = keep.tile([P, PACK], F32, name="two_if_positive")
         sign = keep.tile([P, PACK], F32, name="sign")
         sign_bf = keep.tile([P, PACK], BF16, name="sign_bf")
-        size = keep.tile([P, PACK], F32, name="size")
-        sixteenth = keep.tile([P, PACK], F32, name="sixteenth")
-        nc.gpsimd.tensor_scalar(out=twice[:], in0=gain[:], scalar1=0.0, scalar2=2.0, op0=ALU.is_ge, op1=ALU.mult)
-        nc.gpsimd.tensor_scalar(out=sign[:], in0=twice[:], scalar1=1.0, scalar2=-1.0, op0=ALU.mult, op1=ALU.add)
-        nc.gpsimd.tensor_scalar(out=sign_bf[:], in0=twice[:], scalar1=1.0, scalar2=-1.0, op0=ALU.mult, op1=ALU.add)
-        nc.gpsimd.tensor_scalar(out=sixteenth[:], in0=gain[:], scalar1=0.0625, scalar2=0.0, op0=ALU.mult, op1=ALU.add)
-        nc.gpsimd.tensor_tensor(out=size[:], in0=sixteenth[:], in1=sign[:], op=ALU.mult)
+        factor = keep.tile([P, PACK], F32, name="factor")
+        signed_factor = keep.tile([P, PACK], F32, name="signed_factor")
+        nc.gpsimd.tensor_scalar(out=two_if_positive[:], in0=gain[:], scalar1=0.0, scalar2=2.0, op0=ALU.is_ge, op1=ALU.mult)
+        nc.gpsimd.tensor_scalar(out=sign[:], in0=two_if_positive[:], scalar1=1.0, scalar2=-1.0, op0=ALU.mult, op1=ALU.add)
+        nc.gpsimd.tensor_scalar(out=sign_bf[:], in0=two_if_positive[:], scalar1=1.0, scalar2=-1.0, op0=ALU.mult, op1=ALU.add)
+        nc.gpsimd.tensor_scalar(out=signed_factor[:], in0=gain[:], scalar1=ALPHA, scalar2=0.0, op0=ALU.mult, op1=ALU.add)
+        nc.gpsimd.tensor_tensor(out=factor[:], in0=signed_factor[:], in1=sign[:], op=ALU.mult)
 
-        page = {}
-        for m, at in enumerate((AT_D, AT_D + 4096, AT_PICKED, AT_BYTES)):
-            page[m] = turns.tile([P, U], F32, name=f"page{m}", offset=at)
+        w_raw.append(turns.tile([P, PACK, N // 2], F32, name="w_raw1", offset=AT_D))
+        nc.sync.dma_start(w_raw[1][:], w_rows[:, :, N // 2 :])
+        page = []
+        for m, at in enumerate((AT_D + PAGE_BYTES, AT_PICKED, AT_DEALT, AT_X + PAGE_BYTES)):
+            page.append(turns.tile([P, U], F32, name=f"page{m}", offset=at))
             nc.sync.dma_start(page[m][:], mem[m * P : (m + 1) * P, :])
 
         w_codes = keep.tile([P, N], U32, name="w_codes", align_bytes=64)
         w_plane = keep.tile([P, N], U8, name="w_plane", align_bytes=64)
-        w_bf = [turns.tile([P, N // 2, PACK], BF16, name=f"w_bf{a}", align_bytes=64, offset=AT_X + 2048 * a) for a in range(2)]
+        w_bf = [
+            turns.tile([P, N // 2, PACK], BF16, name=f"w_bf{a}", align_bytes=64, offset=AT_X + TILE_BYTES * a)
+            for a in range(2)
+        ]
         for a in range(2):
-            nc.vector.tensor_copy(out=w_bf[a][:].rearrange("p (c i) t -> p c t i", i=4), in_=w_raw[a][:].rearrange("p t (c i) -> p c t i", i=4))
+            nc.vector.tensor_copy(
+                out=w_bf[a][:].rearrange("p (c e) t -> p c t e", e=4),
+                in_=w_raw[a][:].rearrange("p t (c e) -> p c t e", e=4),
+            )
         for a in range(2):
             ns = slice(a * N // 2, (a + 1) * N // 2)
-            nc.vector.quantize_mx(out=w_codes[:, ns].bitcast(FP8X4), scales=w_plane[:, ns], in_=w_bf[a][:].rearrange("p n t -> p (n t)"))
+            nc.vector.quantize_mx(
+                out=w_codes[:, ns].bitcast(FP8X4), scales=w_plane[:, ns], in_=w_bf[a][:].rearrange("p n t -> p (n t)")
+            )
 
         h_bank = [psum.tile([P, S], F32, name=f"h_bank{t}") for t in range(PACK)]
         for t in range(PACK):
-            cols = slice(t * P, (t + 1) * P)
-            nc.tensor.matmul_mx(out=h_bank[t][:], lhsT=d_codes[:, cols].bitcast(FP8X4), lhsT_scale=planes[:, S + t * P : S + (t + 1) * P],
-                                rhs=x_codes[:].bitcast(FP8X4), rhs_scale=planes[:, :S], start=True, stop=True)
+            nc.tensor.matmul_mx(
+                out=h_bank[t][:],
+                lhsT=d_codes[:, t * P : (t + 1) * P].bitcast(FP8X4),
+                lhsT_scale=planes[:, S + t * P : S + (t + 1) * P],
+                rhs=x_codes[:].bitcast(FP8X4),
+                rhs_scale=planes[:, :S],
+                start=True,
+                stop=True,
+            )
 
-        gate = [turns.tile([P, S + SPARE], F32, name=f"gate{t}", offset=AT_GATE + 4 * (S + SPARE) * (PACK - 1 - t)) for t in range(PACK)]
+        gate = [
+            turns.tile([P, S + SPARE], F32, name=f"gate{t}", offset=AT_GATE + 4 * (S + SPARE) * (PACK - 1 - t))
+            for t in range(PACK)
+        ]
         for t in range(PACK):
             nc.gpsimd.memset(gate[t][:, S:], 0.0)
-        h_sized = [keep.tile([P, S], F32, name=f"h_sized{t}") for t in range(PACK)]
-        st = keep.tile([P, PACK, S], F32, name="st")
+        h_scaled = [keep.tile([P, S], F32, name=f"h_scaled{t}") for t in range(PACK)]
+        st_scaled = keep.tile([P, PACK, S], F32, name="st_scaled")
         st_n1 = keep.tile([P, PACK, S], F32, name="st_n1")
         for t in range(PACK):
-            nc.scalar.activation(out=gate[t][:, :S], in_=h_bank[t][:], func=ACT.Sigmoid, scale=0.0625)
-            nc.scalar.activation(out=h_sized[t][:], in_=h_bank[t][:], func=ACT.Copy, scale=size[:, t : t + 1])
+            nc.scalar.activation(out=gate[t][:, :S], in_=h_bank[t][:], func=ACT.Sigmoid, scale=ALPHA)
+            nc.scalar.activation(out=h_scaled[t][:], in_=h_bank[t][:], func=ACT.Copy, scale=factor[:, t : t + 1])
         for t in range(PACK):
-            nc.vector.tensor_tensor(out=st[:, t, :], in0=gate[t][:].indirect(n1_sb[:]), in1=h_sized[t][:], op=ALU.mult)
+            nc.vector.tensor_tensor(out=st_scaled[:, t, :], in0=gate[t][:].indirect(n1_sb[:]), in1=h_scaled[t][:], op=ALU.mult)
         for a in range(2):
             for t in range(PACK):
-                fetch(nc, (t, a) != (PACK - 1, 0), st_n1[:, t, half_cols(a)], st[:, t, :].indirect(half_list(n1_sb, a)))
+                fetched = st_n1[:, t, half_cols(a)]
+                window = st_scaled[:, t, :].indirect(half_list(n1_sb, a))
+                if (t, a) == (PACK - 1, 0):
+                    nc.vector.tensor_copy(out=fetched, in_=window)
+                else:
+                    scalar_move(nc, fetched, window)
 
         z_codes = keep.tile([P, S], U32, name="z_codes", align_bytes=64)
         z_plane = keep.tile([P, S], U8, name="z_plane", align_bytes=64)
-        old = [turns.tile([P, 2, S], F32, name="old0", offset=AT_GATE - 4096 + 64)]
-        for m in range(2):
-            fetch(nc, True, old[m // 2][:, m % 2, :], page[m][:].indirect(n2_sb[:]))
+        old = [turns.tile([P, 2, S], F32, name="old0", offset=AT_OLD_01)]
+        for c in range(2):
+            scalar_move(nc, old[0][:, c, :], page[c][:].indirect(n2_sb[:]))
+
         h2_bank = [[psum.tile([P, 2, HALF], F32, name=f"h2_bank{a}{b}") for b in range(2)] for a in range(2)]
-        share = keep.tile([P, 4, S], F32, name="share")
-        gap = keep.tile([P, 4, S], F32, name="gap")
-        step = keep.tile([P, 4, S], F32, name="step")
-        new = keep.tile([P, 3, S], F32, name="new")
+        share = keep.tile([P, PAGES, S], F32, name="share")
+        gap = keep.tile([P, PAGES, S], F32, name="gap")
+        step = keep.tile([P, PAGES, S], F32, name="step")
+        new = keep.tile([P, PAGES - 1, S], F32, name="new")
         for a in range(2):
             js = half_cols(a)
-            z_size = keep.tile([P, HALF, PACK], BF16, name="z_size", align_bytes=64)
-            nc.vector.tensor_tensor(out=z_size[:].rearrange("p (c i) t -> p c t i", i=2),
-                                    in0=st[:, :, js].rearrange("p t (c i) -> p c t i", i=2),
-                                    in1=st_n1[:, :, js].rearrange("p t (c i) -> p c t i", i=2), op=ALU.max)
-            z_bf = turns.tile([P, HALF, PACK], BF16, name=f"z_bf{a}", align_bytes=64, offset=AT_Z + 4096 * a)
-            nc.vector.tensor_tensor(out=z_bf[:], in0=z_size[:],
-                                    in1=sign_bf[:].rearrange("p (o t) -> p o t", o=1).to_broadcast([P, HALF, PACK]), op=ALU.mult)
-            nc.vector.quantize_mx(out=z_codes[:, js].bitcast(FP8X4), scales=z_plane[:, js], in_=z_bf[:].rearrange("p j t -> p (j t)"))
-            for m in range(4):
+            z_unsigned = keep.tile([P, HALF, PACK], BF16, name="z_unsigned", align_bytes=64)
+            nc.vector.tensor_tensor(
+                out=z_unsigned[:].rearrange("p (c e) t -> p c t e", e=2),
+                in0=st_scaled[:, :, js].rearrange("p t (c e) -> p c t e", e=2),
+                in1=st_n1[:, :, js].rearrange("p t (c e) -> p c t e", e=2),
+                op=ALU.max,
+            )
+            z_bf = turns.tile([P, HALF, PACK], BF16, name=f"z_bf{a}", align_bytes=64, offset=AT_Z + PAGE_BYTES * a)
+            nc.vector.tensor_tensor(
+                out=z_bf[:],
+                in0=z_unsigned[:],
+                in1=sign_bf[:].rearrange("p (o t) -> p o t", o=1).to_broadcast([P, HALF, PACK]),
+                op=ALU.mult,
+            )
+            nc.vector.quantize_mx(
+                out=z_codes[:, js].bitcast(FP8X4), scales=z_plane[:, js], in_=z_bf[:].rearrange("p j t -> p (j t)")
+            )
+            for m in range(PAGES):
                 cols = slice(m * P, (m + 1) * P)
-                nc.tensor.matmul_mx(out=h2_bank[a][m // 2][:, m % 2, :], lhsT=w_codes[:, cols].bitcast(FP8X4), lhsT_scale=w_plane[:, cols],
-                                    rhs=z_codes[:, js].bitcast(FP8X4), rhs_scale=z_plane[:, js], start=True, stop=True)
+                nc.tensor.matmul_mx(
+                    out=h2_bank[a][m // 2][:, m % 2, :],
+                    lhsT=w_codes[:, cols].bitcast(FP8X4),
+                    lhsT_scale=w_plane[:, cols],
+                    rhs=z_codes[:, js].bitcast(FP8X4),
+                    rhs_scale=z_plane[:, js],
+                    start=True,
+                    stop=True,
+                )
             for b in range(2):
                 nc.scalar.activation(out=share[:, 2 * b : 2 * b + 2, js], in_=h2_bank[a][b][:], func=ACT.Sigmoid)
         old.append(turns.tile([P, 2, S], F32, name="old1", offset=AT_Z))
-        for m in range(2, 4):
-            fetch(nc, True, old[1][:, m % 2, :], page[m][:].indirect(n2_sb[:]))
+        for c in range(2):
+            scalar_move(nc, old[1][:, c, :], page[2 + c][:].indirect(n2_sb[:]))
+
         for b in range(2):
             ms = slice(2 * b, 2 * b + 2)
             for a in range(2):
@@ -176,12 +232,15 @@ def tile_picked_hpqtwicppaget_none_p_kernel(tc, x_words, x_scales, d_words, d_sc
                     nc.vector.tensor_tensor(out=new[:, ms, js], in0=step[:, ms, js], in1=old[b][:, :, js], op=ALU.add)
         cut = S - SCALAR_TAIL
         nc.vector.tensor_tensor(out=new[:, 2, cut:], in0=step[:, 2, cut:], in1=old[1][:, 0, cut:], op=ALU.add)
+
         for m in range(2):
             for a in range(2):
-                nc.scalar.activation(out=page[m][:].indirect(half_list(n2_sb, a)), in_=new[:, m, half_cols(a)], func=ACT.Copy)
+                scalar_move(nc, page[m][:].indirect(half_list(n2_sb, a)), new[:, m, half_cols(a)])
             nc.sync.dma_start(out[m * P : (m + 1) * P, :], page[m][:])
-        nc.vector.tensor_tensor(out=page[2][:].indirect(n2_sb[:, : cut // 16]), in0=step[:, 2, :cut], in1=old[1][:, 0, :cut], op=ALU.add)
+        nc.vector.tensor_tensor(
+            out=page[2][:].indirect(n2_sb[:, : cut // 16]), in0=step[:, 2, :cut], in1=old[1][:, 0, :cut], op=ALU.add
+        )
         nc.vector.tensor_tensor(out=page[3][:].indirect(n2_sb[:]), in0=step[:, 3, :], in1=old[1][:, 1, :], op=ALU.add)
-        nc.scalar.activation(out=page[2][:].indirect(n2_sb[:, cut // 16 :]), in_=new[:, 2, cut:], func=ACT.Copy)
-        for m in range(2, 4):
+        scalar_move(nc, page[2][:].indirect(n2_sb[:, cut // 16 :]), new[:, 2, cut:])
+        for m in range(2, PAGES):
             nc.sync.dma_start(out[m * P : (m + 1) * P, :], page[m][:])

from contextlib import ExitStack

import concourse.mybir as mybir

F32 = mybir.dt.float32
BF16 = mybir.dt.bfloat16
I32 = mybir.dt.int32
U32 = mybir.dt.uint32
U16 = mybir.dt.uint16
U8 = mybir.dt.uint8
FP8X4 = mybir.dt.float8_e4m3fn_x4
ALU = mybir.AluOpType
ACT = mybir.ActivationFunctionType

P = 128
PACK = 4
PAGES = 4
K, T, S, N, G, H, U = 512, 2048, 512, 512, 2048, 512, 1024
HALF = S // 2
LIST_COLS = S // 16
ALPHA = 0.0625
SPARE = 16
SCALAR_TAIL = 192
FLOPS = 2 * K * H * S + 2 * H * N * S

TILE_BYTES = 4 * S
PAGE_BYTES = 4 * U
AT_D = 0
AT_PICKED = 2 * PAGE_BYTES
AT_DEALT = 3 * PAGE_BYTES
AT_X = 4 * PAGE_BYTES
AT_GATE = 8 * PAGE_BYTES
AT_OLD_01 = AT_GATE - PAGE_BYTES + 64
AT_Z = 12 * PAGE_BYTES


def half_cols(a):
    return slice(a * HALF, (a + 1) * HALF)


def half_list(lst, a):
    return lst[:, a * LIST_COLS // 2 : (a + 1) * LIST_COLS // 2]


def scalar_move(nc, out, in_):
    nc.scalar.activation(out=out, in_=in_, func=ACT.Copy)


def tile_picked_hpqtwicppaget_none_p_kernel(
    tc, x_words, x_scales, d_words, d_scales, gn, w1, mem, offs, k1, n1, n2, out
):
    nc = tc.nc
    with ExitStack() as ctx:
        keep = ctx.enter_context(tc.tile_pool(name="keep", bufs=1))
        turns = ctx.enter_context(tc.tile_pool(name="turns", bufs=1))
        psum = ctx.enter_context(tc.psum_pool(name="psum", bufs=1))

        offs_sb = keep.tile([P, LIST_COLS], U16, name="offs_sb")
        k1_sb = keep.tile([P, LIST_COLS], U16, name="k1_sb")
        n1_sb = keep.tile([P, LIST_COLS], U16, name="n1_sb")
        n2_sb = keep.tile([P, LIST_COLS], U16, name="n2_sb")

        x_scale_tab = keep.tile([P, T], U8, name="x_scale_tab", align_bytes=64)
        d_scale_tab = keep.tile([P, G], U8, name="d_scale_tab", align_bytes=64)
        planes = keep.tile([P, S + H], U8, name="planes", align_bytes=64)
        nc.vector.memset(d_scale_tab[:].bitcast(I32), 0)
        nc.vector.memset(x_scale_tab[:].bitcast(I32), 0)
        nc.vector.memset(planes[:].bitcast(I32), 0)

        d_word_tab = turns.tile([P, G], U32, name="d_word_tab", offset=AT_D)
        x_word_tab = turns.tile([P, T], U32, name="x_word_tab", offset=AT_X)
        nc.sync.dma_start(k1_sb[:], k1)
        nc.sync.dma_start(offs_sb[:], offs)
        nc.sync.dma_start(d_scale_tab[0:P:8, :].bitcast(I32), d_scales[0].bitcast(I32))
        nc.sync.dma_start(x_scale_tab[0:P:8, :].bitcast(I32), x_scales[0].bitcast(I32))
        nc.sync.dma_start(n1_sb[:], n1)
        nc.sync.dma_start(n2_sb[:], n2)
        nc.sync.dma_start(d_word_tab[:].bitcast(I32), d_words[0].rearrange("p n t -> p (n t)").bitcast(I32))
        nc.sync.dma_start(x_word_tab[:].bitcast(I32), x_words[0].rearrange("p n t -> p (n t)").bitcast(I32))
        w_rows = w1.rearrange("(p t) n -> p t n", t=PACK)
        w_raw = [keep.tile([P, PACK, N // 2], F32, name="w_raw0")]
        nc.sync.dma_start(w_raw[0][:], w_rows[:, :, : N // 2])
        gain = keep.tile([P, PACK], F32, name="gain")
        nc.gpsimd.dma_start(gain[:], gn.rearrange("(p t) o -> p (t o)", t=PACK))

        picked_bytes = turns.tile([P, S + H], U8, name="picked_bytes", align_bytes=64, offset=AT_PICKED)
        dealt_bytes = turns.tile([P, S + H], U8, name="dealt_bytes", align_bytes=64, offset=AT_DEALT)
        nc.vector.tensor_copy(out=picked_bytes[:, S:], in_=d_scale_tab[:].indirect(k1_sb[:]))
        nc.vector.tensor_copy(out=picked_bytes[:, :S], in_=x_scale_tab[:].indirect(offs_sb[:]))
        nc.vector.tensor_copy(
            out=dealt_bytes[:, S:].rearrange("p (t c) -> p t c", t=PACK),
            in_=picked_bytes[:, S:].rearrange("p (c t) -> p t c", t=PACK),
        )
        nc.vector.tensor_copy(out=dealt_bytes[:, :S].bitcast(I32), in_=picked_bytes[:, :S].bitcast(I32))
        for r in range(4):
            nc.sync.dma_start(planes[r:P:32, :].bitcast(I32), dealt_bytes[8 * r : P : 32, :].bitcast(I32))

        d_picked = turns.tile([P, H], U32, name="d_picked", offset=AT_PICKED)
        nc.vector.tensor_copy(out=d_picked[:], in_=d_word_tab[:].indirect(k1_sb[:]))
        d_codes = keep.tile([P, H], U32, name="d_codes", align_bytes=64)
        nc.vector.tensor_copy(
            out=d_codes[:].rearrange("p (t c e) -> p c t e", t=PACK, e=4),
            in_=d_picked[:].rearrange("p (c e t) -> p c t e", t=PACK, e=4),
        )
        x_codes = keep.tile([P, S], U32, name="x_codes", align_bytes=64)
        nc.vector.tensor_copy(out=x_codes[:], in_=x_word_tab[:].indirect(offs_sb[:]))

        two_if_positive = keep.tile([P, PACK], F32, name="two_if_positive")
        sign = keep.tile([P, PACK], F32, name="sign")
        sign_bf = keep.tile([P, PACK], BF16, name="sign_bf")
        factor = keep.tile([P, PACK], F32, name="factor")
        signed_factor = keep.tile([P, PACK], F32, name="signed_factor")
        nc.gpsimd.tensor_scalar(out=two_if_positive[:], in0=gain[:], scalar1=0.0, scalar2=2.0, op0=ALU.is_ge, op1=ALU.mult)
        nc.gpsimd.tensor_scalar(out=sign[:], in0=two_if_positive[:], scalar1=1.0, scalar2=-1.0, op0=ALU.mult, op1=ALU.add)
        nc.gpsimd.tensor_scalar(out=sign_bf[:], in0=two_if_positive[:], scalar1=1.0, scalar2=-1.0, op0=ALU.mult, op1=ALU.add)
        nc.gpsimd.tensor_scalar(out=signed_factor[:], in0=gain[:], scalar1=ALPHA, scalar2=0.0, op0=ALU.mult, op1=ALU.add)
        nc.gpsimd.tensor_tensor(out=factor[:], in0=signed_factor[:], in1=sign[:], op=ALU.mult)

        w_raw.append(turns.tile([P, PACK, N // 2], F32, name="w_raw1", offset=AT_D))
        nc.sync.dma_start(w_raw[1][:], w_rows[:, :, N // 2 :])
        page = []
        for m, at in enumerate((AT_D + PAGE_BYTES, AT_PICKED, AT_DEALT, AT_X + PAGE_BYTES)):
            page.append(turns.tile([P, U], F32, name=f"page{m}", offset=at))
            nc.sync.dma_start(page[m][:], mem[m * P : (m + 1) * P, :])

        w_codes = keep.tile([P, N], U32, name="w_codes", align_bytes=64)
        w_plane = keep.tile([P, N], U8, name="w_plane", align_bytes=64)
        w_bf = [
            turns.tile([P, N // 2, PACK], BF16, name=f"w_bf{a}", align_bytes=64, offset=AT_X + TILE_BYTES * a)
            for a in range(2)
        ]
        for a in range(2):
            nc.vector.tensor_copy(
                out=w_bf[a][:].rearrange("p (c e) t -> p c t e", e=4),
                in_=w_raw[a][:].rearrange("p t (c e) -> p c t e", e=4),
            )
        for a in range(2):
            ns = slice(a * N // 2, (a + 1) * N // 2)
            nc.vector.quantize_mx(
                out=w_codes[:, ns].bitcast(FP8X4), scales=w_plane[:, ns], in_=w_bf[a][:].rearrange("p n t -> p (n t)")
            )

        h_bank = [psum.tile([P, S], F32, name=f"h_bank{t}") for t in range(PACK)]
        for t in range(PACK):
            nc.tensor.matmul_mx(
                out=h_bank[t][:],
                lhsT=d_codes[:, t * P : (t + 1) * P].bitcast(FP8X4),
                lhsT_scale=planes[:, S + t * P : S + (t + 1) * P],
                rhs=x_codes[:].bitcast(FP8X4),
                rhs_scale=planes[:, :S],
                start=True,
                stop=True,
            )

        gate = [
            turns.tile([P, S + SPARE], F32, name=f"gate{t}", offset=AT_GATE + 4 * (S + SPARE) * (PACK - 1 - t))
            for t in range(PACK)
        ]
        for t in range(PACK):
            nc.gpsimd.memset(gate[t][:, S:], 0.0)
        h_scaled = [keep.tile([P, S], F32, name=f"h_scaled{t}") for t in range(PACK)]
        st_scaled = keep.tile([P, PACK, S], F32, name="st_scaled")
        st_n1 = keep.tile([P, PACK, S], F32, name="st_n1")
        for t in range(PACK):
            nc.scalar.activation(out=gate[t][:, :S], in_=h_bank[t][:], func=ACT.Sigmoid, scale=ALPHA)
            nc.scalar.activation(out=h_scaled[t][:], in_=h_bank[t][:], func=ACT.Copy, scale=factor[:, t : t + 1])
        for t in range(PACK):
            nc.vector.tensor_tensor(out=st_scaled[:, t, :], in0=gate[t][:].indirect(n1_sb[:]), in1=h_scaled[t][:], op=ALU.mult)
        for a in range(2):
            for t in range(PACK):
                fetched = st_n1[:, t, half_cols(a)]
                window = st_scaled[:, t, :].indirect(half_list(n1_sb, a))
                if (t, a) == (PACK - 1, 0):
                    nc.vector.tensor_copy(out=fetched, in_=window)
                else:
                    scalar_move(nc, fetched, window)

        z_codes = keep.tile([P, S], U32, name="z_codes", align_bytes=64)
        z_plane = keep.tile([P, S], U8, name="z_plane", align_bytes=64)
        old = [turns.tile([P, 2, S], F32, name="old0", offset=AT_OLD_01)]
        for c in range(2):
            scalar_move(nc, old[0][:, c, :], page[c][:].indirect(n2_sb[:]))

        h2_bank = [[psum.tile([P, 2, HALF], F32, name=f"h2_bank{a}{b}") for b in range(2)] for a in range(2)]
        share = keep.tile([P, PAGES, S], F32, name="share")
        gap = keep.tile([P, PAGES, S], F32, name="gap")
        step = keep.tile([P, PAGES, S], F32, name="step")
        new = keep.tile([P, PAGES - 1, S], F32, name="new")
        for a in range(2):
            js = half_cols(a)
            z_unsigned = keep.tile([P, HALF, PACK], BF16, name="z_unsigned", align_bytes=64)
            nc.vector.tensor_tensor(
                out=z_unsigned[:].rearrange("p (c e) t -> p c t e", e=2),
                in0=st_scaled[:, :, js].rearrange("p t (c e) -> p c t e", e=2),
                in1=st_n1[:, :, js].rearrange("p t (c e) -> p c t e", e=2),
                op=ALU.max,
            )
            z_bf = turns.tile([P, HALF, PACK], BF16, name=f"z_bf{a}", align_bytes=64, offset=AT_Z + PAGE_BYTES * a)
            nc.vector.tensor_tensor(
                out=z_bf[:],
                in0=z_unsigned[:],
                in1=sign_bf[:].rearrange("p (o t) -> p o t", o=1).to_broadcast([P, HALF, PACK]),
                op=ALU.mult,
            )
            nc.vector.quantize_mx(
                out=z_codes[:, js].bitcast(FP8X4), scales=z_plane[:, js], in_=z_bf[:].rearrange("p j t -> p (j t)")
            )
            for m in range(PAGES):
                cols = slice(m * P, (m + 1) * P)
                nc.tensor.matmul_mx(
                    out=h2_bank[a][m // 2][:, m % 2, :],
                    lhsT=w_codes[:, cols].bitcast(FP8X4),
                    lhsT_scale=w_plane[:, cols],
                    rhs=z_codes[:, js].bitcast(FP8X4),
                    rhs_scale=z_plane[:, js],
                    start=True,
                    stop=True,
                )
            for b in range(2):
                nc.scalar.activation(out=share[:, 2 * b : 2 * b + 2, js], in_=h2_bank[a][b][:], func=ACT.Sigmoid)
        old.append(turns.tile([P, 2, S], F32, name="old1", offset=AT_Z))
        for c in range(2):
            scalar_move(nc, old[1][:, c, :], page[2 + c][:].indirect(n2_sb[:]))

        for b in range(2):
            ms = slice(2 * b, 2 * b + 2)
            for a in range(2):
                js = half_cols(a)
                nc.vector.tensor_tensor(out=gap[:, ms, js], in0=h2_bank[a][b][:], in1=old[b][:, :, js], op=ALU.subtract)
                nc.vector.tensor_tensor(out=step[:, ms, js], in0=gap[:, ms, js], in1=share[:, ms, js], op=ALU.mult)
                if b == 0:
                    nc.vector.tensor_tensor(out=new[:, ms, js], in0=step[:, ms, js], in1=old[b][:, :, js], op=ALU.add)
        cut = S - SCALAR_TAIL
        nc.vector.tensor_tensor(out=new[:, 2, cut:], in0=step[:, 2, cut:], in1=old[1][:, 0, cut:], op=ALU.add)

        for m in range(2):
            for a in range(2):
                scalar_move(nc, page[m][:].indirect(half_list(n2_sb, a)), new[:, m, half_cols(a)])
            nc.sync.dma_start(out[m * P : (m + 1) * P, :], page[m][:])
        nc.vector.tensor_tensor(
            out=page[2][:].indirect(n2_sb[:, : cut // 16]), in0=step[:, 2, :cut], in1=old[1][:, 0, :cut], op=ALU.add
        )
        nc.vector.tensor_tensor(out=page[3][:].indirect(n2_sb[:]), in0=step[:, 3, :], in1=old[1][:, 1, :], op=ALU.add)
        scalar_move(nc, page[2][:].indirect(n2_sb[:, cut // 16 :]), new[:, 2, cut:])
        for m in range(2, PAGES):
            nc.sync.dma_start(out[m * P : (m + 1) * P, :], page[m][:])
